import numpy as np
import ml_dtypes


def mxq(x, axis, fmt="e4m3"):
    dtype, down = {"e4m3": (ml_dtypes.float8_e4m3fn, 7), "e5m2": (ml_dtypes.float8_e5m2, 14)}[fmt]
    v = np.moveaxis(np.asarray(x, np.float32).astype(ml_dtypes.bfloat16).astype(np.float64), axis, -1)
    blocks = v.reshape(v.shape[:-1] + (-1, 32))
    amax = np.abs(blocks).max(-1, keepdims=True)
    byte = np.maximum(np.where(amax > 0, np.frexp(amax)[1] - 1 + 127, 0) - down, 1)
    scale = np.exp2(byte - 127.0)
    codes = (blocks / scale).astype(np.float32).astype(dtype).astype(np.float64)
    return np.moveaxis((codes * scale).reshape(v.shape), -1, axis)


WIDE = False


def mx_kscale(k, group=512):
    if not WIDE:
        return np.ones(k)
    levels = np.array([10, -10, 5, -5, 0])
    if group != 512:
        return np.exp2(np.random.permutation(np.resize(levels, k // group))).repeat(group)
    if k % 512:
        return np.exp2(np.random.permutation(np.resize(levels, k // 32))).repeat(32)
    a = np.empty((k // 512, 16))
    for p in range(k // 512):
        a[p, :8] = np.random.permutation(np.resize(levels, 8))
        for g in range(8):
            far = levels[np.abs(levels - a[p, g]) >= 10]
            a[p, g + 8] = far[np.random.randint(len(far))]
    return np.exp2(a.ravel()).repeat(32)


def f64(x):
    return np.asarray(x).astype(np.float64)


E2M1 = np.array([0.0, 0.5, 1.0, 1.5, 2.0, 3.0, 4.0, 6.0, -0.0, -0.5, -1.0, -1.5, -2.0, -3.0, -4.0, -6.0])


def pack_group(w):
    k, n = w.shape
    w = f64(np.asarray(w, np.float32).astype(ml_dtypes.bfloat16)).reshape(k // 32, 32, n)
    amax = np.abs(w).max(1)
    mant, ex = np.frexp(amax / 6.0)
    byte = np.clip(np.where(amax > 0, np.where(mant > 0.5, ex, ex - 1) + 127, 1), 1, 254)
    scaled = (w * np.exp2(127.0 - byte)[:, None, :]).reshape(k, n).astype(np.float32)
    c = np.ascontiguousarray(scaled.reshape(k // 4, 4, n).transpose(0, 2, 1)).astype(ml_dtypes.float4_e2m1fn).view(np.uint8) & 0xF
    return np.ascontiguousarray((c[..., 0::2] | (c[..., 1::2] << 4)).reshape(k // 4, 2 * n)), byte.astype(np.uint8)


def unpack_group(words, scales):
    p, n = words.shape[0], scales.shape[1]
    words = np.ascontiguousarray(words).reshape(p, n, 2)
    nib = np.empty((p, n, 4), np.uint8)
    nib[..., 0::2] = words & 0xF
    nib[..., 1::2] = words >> 4
    return E2M1[nib].transpose(0, 2, 1).reshape(4 * p, n) * np.repeat(np.exp2(scales.astype(np.float64) - 127.0), 32, axis=0)


def silu(v):
    return v / (1.0 + np.exp(-v))


G, D, M, N = 4, 256, 256, 512


def setup_inputs():
    n = np.random.standard_normal
    s = mx_kscale(D, 0)[:, None]
    w_ = [pack_group(w) for w in n((G, D, M)) / np.sqrt(D) / s]
    return {
        "x": (n((G, D, N)) * s).astype(np.float32),
        "w_words": np.stack([w[0] for w in w_]),
        "w_scales": np.stack([w[1] for w in w_]),
        "b": (0.5 * n((G, M, 1))).astype(np.float32),
        "r": n((G, M, N)).astype(np.float32),
    }


def reference(x, w_words, w_scales, b, r):
    xq = mxq(f64(x), 1, "e4m3")
    y = np.stack([unpack_group(w_words[g], w_scales[g]) for g in range(G)]).transpose(0, 2, 1) @ xq
    y = y + f64(b)
    y = silu(y)
    y = y + f64(r)
    return y

@@ -1,0 +1,121 @@
+from contextlib import ExitStack
+
+import concourse.mybir as mybir
+
+F32 = mybir.dt.float32
+BF16 = mybir.dt.bfloat16
+I32 = mybir.dt.int32
+U32 = mybir.dt.uint32
+U8 = mybir.dt.uint8
+FP8X4 = mybir.dt.float8_e4m3fn_x4
+FP4X4 = mybir.dt.float4_e2m1fn_x4
+SILU = mybir.ActivationFunctionType.Silu
+ADD = mybir.AluOpType.add
+
+G, D, M, N = 4, 256, 256, 512
+FLOPS = 2 * G * D * M * N
+P = 128
+PACK = 4
+ROWS = D // PACK
+SIDE = P // ROWS
+PAIRS = G // SIDE
+HALVES = M // P
+VECTOR_COLUMNS = 352
+
+
+def tile_rows_glin_silu_bias_res_kernel(tc, x, w_words, w_scales, b, r, out):
+    nc = tc.nc
+    with ExitStack() as ctx:
+        sb = ctx.enter_context(tc.tile_pool(name="sb", bufs=1))
+        ps = ctx.enter_context(tc.psum_pool(name="ps", bufs=1))
+        ctx.enter_context(tc.manual_schedule())
+
+        words_in = sb.tile([P, PAIRS, 2 * M], U8, align_bytes=64)
+        words = sb.tile([P, HALVES, PAIRS, 2 * P], U8, align_bytes=64)
+        wscale_in = sb.tile([P, PAIRS, M], U8, align_bytes=64)
+        wscale = sb.tile([P, HALVES, PAIRS, P], U8, align_bytes=64)
+        bias = sb.tile([P, G, 8], F32)
+        warm = sb.tile([P, 8], F32)
+        warm_out = sb.tile([P, 8], F32)
+        x_in = [sb.tile([P, PACK, N], F32, name="x_in%d" % s, align_bytes=64) for s in range(PAIRS)]
+        x_bf = [sb.tile([P, N, PACK], BF16, name="x_bf%d" % s, align_bytes=64) for s in range(PAIRS)]
+        codes = [sb.tile([P, N], U32, name="codes%d" % s, align_bytes=64) for s in range(PAIRS)]
+        xscale = [sb.tile([P, N], U8, name="xscale%d" % s, align_bytes=64) for s in range(PAIRS)]
+        r_in = sb.tile([P, G, HALVES, N], F32)
+        act = sb.tile([P, G, HALVES, N], F32)
+        res = sb.tile([P, G, HALVES, N], F32)
+        acc = [[ps.tile([P, N], F32, name="acc%d_%d" % (g, h)) for h in range(HALVES)] for g in range(G)]
+
+        x_v = x.rearrange("(s c) (p j) n -> s (c p) j n", c=SIDE, j=PACK)
+        r_v = r.rearrange("g (p h) n -> p g h n", h=HALVES)
+        out_v = out.rearrange("g (p h) n -> p g h n", h=HALVES)
+        scale_v = w_scales.rearrange("(s c) (q i) m -> i (c q) s m", c=SIDE, i=4)
+
+        nc.vector.memset(wscale_in[:].bitcast(I32), 0)
+        nc.vector.memset(warm[:], 0.0)
+
+        nc.sync.dma_start(
+            out=words_in[:].bitcast(I32),
+            in_=w_words.rearrange("(s c) p y -> (c p) s y", c=SIDE).bitcast(I32),
+        )
+        for s in range(PAIRS):
+            nc.sync.dma_start(out=x_in[s][:], in_=x_v[s])
+        for lo, hi in ((0, 1), (1, 2), (2, 4)):
+            nc.sync.dma_start(out=r_in[:, lo:hi], in_=r_v[:, lo:hi])
+
+        for i in range(4):
+            nc.scalar.dma_start(out=wscale_in[i:P:32].bitcast(I32), in_=scale_v[i].bitcast(I32))
+        nc.scalar.activation(out=warm_out[:], in_=warm[:], func=SILU)
+        nc.scalar.dma_start(out=bias[:, :, 0:HALVES], in_=b.rearrange("g (p h) o -> p g (h o)", h=HALVES))
+
+        def interleave(s, engine_copy, lo, hi):
+            engine_copy(
+                out=x_bf[s][:, lo:hi, :].rearrange("p (c i) t -> p c t i", i=4),
+                in_=x_in[s][:, :, lo:hi].rearrange("p t (c i) -> p c t i", i=4),
+            )
+
+        def quantize(s):
+            nc.vector.quantize_mx(
+                out=codes[s][:].bitcast(FP8X4),
+                scales=xscale[s][:],
+                in_=x_bf[s][:].rearrange("p n t -> p (n t)"),
+            )
+
+        def multiply(s):
+            for h in range(HALVES):
+                for c in range(SIDE):
+                    rows = slice(ROWS * c, ROWS * (c + 1))
+                    nc.tensor.matmul_mx(
+                        out=acc[SIDE * s + c][h][:],
+                        lhsT=words[rows, h, s, :].bitcast(FP4X4),
+                        lhsT_scale=wscale[rows, h, s, :],
+                        rhs=codes[s][rows, :].bitcast(FP8X4),
+                        rhs_scale=xscale[s][rows, :],
+                        start=True,
+                        stop=True,
+                    )
+
+        def finish(g):
+            for h in range(HALVES):
+                nc.scalar.activation(out=act[:, g, h, :], in_=acc[g][h][:], func=SILU, bias=bias[:, g, h : h + 1])
+                nc.vector.tensor_tensor(out=res[:, g, h, :], in0=act[:, g, h, :], in1=r_in[:, g, h, :], op=ADD)
+            nc.sync.dma_start(out=out_v[:, g], in_=res[:, g])
+
+        nc.vector.tensor_copy(
+            out=words[:].rearrange("p h s (q y) -> p h (s q) y", y=2),
+            in_=words_in[:].rearrange("p s (q h y) -> p h (s q) y", h=HALVES, y=2),
+        )
+        interleave(0, nc.vector.tensor_copy, 0, VECTOR_COLUMNS)
+        interleave(0, nc.scalar.copy, VECTOR_COLUMNS, N)
+        nc.vector.tensor_copy(
+            out=wscale[:].rearrange("p h s q -> p h (s q)"),
+            in_=wscale_in[:].rearrange("p s (q h) -> p h (s q)", h=HALVES),
+        )
+        quantize(0)
+        multiply(0)
+        interleave(1, nc.vector.tensor_copy, 0, VECTOR_COLUMNS)
+        interleave(1, nc.scalar.copy, VECTOR_COLUMNS, N)
+        quantize(1)
+        multiply(1)
+        for g in range(G):
+            finish(g)

@@ -34,7 +34,9 @@ def tile_rows_glin_silu_bias_res_kernel(tc, x, w_words, w_scales, b, r, out):
         words = sb.tile([P, HALVES, PAIRS, 2 * P], U8, align_bytes=64)
         wscale_in = sb.tile([P, PAIRS, M], U8, align_bytes=64)
         wscale = sb.tile([P, HALVES, PAIRS, P], U8, align_bytes=64)
-        bias = sb.tile([P, G, 8], F32)
+        bias_in = sb.tile([P, 64], F32, align_bytes=64)
+        bias_dealt = sb.tile([P, HALVES, 32], F32, align_bytes=64)
+        bias = sb.tile([P, HALVES, 32], F32, align_bytes=64)
         warm = sb.tile([P, 8], F32)
         warm_out = sb.tile([P, 8], F32)
         x_in = [sb.tile([P, PACK, N], F32, name="x_in%d" % s, align_bytes=64) for s in range(PAIRS)]
@@ -53,20 +55,21 @@ def tile_rows_glin_silu_bias_res_kernel(tc, x, w_words, w_scales, b, r, out):
 
         nc.vector.memset(wscale_in[:].bitcast(I32), 0)
         nc.vector.memset(warm[:], 0.0)
+        nc.vector.memset(bias_in[:], 0.0)
 
         nc.sync.dma_start(
             out=words_in[:].bitcast(I32),
             in_=w_words.rearrange("(s c) p y -> (c p) s y", c=SIDE).bitcast(I32),
         )
-        for s in range(PAIRS):
-            nc.sync.dma_start(out=x_in[s][:], in_=x_v[s])
-        for lo, hi in ((0, 1), (1, 2), (2, 4)):
-            nc.sync.dma_start(out=r_in[:, lo:hi], in_=r_v[:, lo:hi])
-
+        nc.sync.dma_start(out=x_in[0][:], in_=x_v[0])
         for i in range(4):
-            nc.scalar.dma_start(out=wscale_in[i:P:32].bitcast(I32), in_=scale_v[i].bitcast(I32))
+            nc.sync.dma_start(out=wscale_in[i:P:32].bitcast(I32), in_=scale_v[i].bitcast(I32))
+        nc.sync.dma_start(out=bias_in[0:P:8, :], in_=b.rearrange("g (q j) o -> q g (j o)", q=4))
+        for lo in (0, 2):
+            nc.sync.dma_start(out=x_in[1][:, lo : lo + 2], in_=x_v[1][:, lo : lo + 2])
+        for lo, hi in ((0, 1), (1, 2), (2, 3), (3, 4)):
+            nc.sync.dma_start(out=r_in[:, lo:hi], in_=r_v[:, lo:hi])
         nc.scalar.activation(out=warm_out[:], in_=warm[:], func=SILU)
-        nc.scalar.dma_start(out=bias[:, :, 0:HALVES], in_=b.rearrange("g (p h) o -> p g (h o)", h=HALVES))
 
         def interleave(s, engine_copy, lo, hi):
             engine_copy(
@@ -74,16 +77,19 @@ def tile_rows_glin_silu_bias_res_kernel(tc, x, w_words, w_scales, b, r, out):
                 in_=x_in[s][:, :, lo:hi].rearrange("p t (c i) -> p c t i", i=4),
             )
 
-        def quantize(s):
+        def pair_copy(engine_copy, t, lo, hi):
+            engine_copy(out=x_bf[1][:, lo:hi, t : t + 2], in_=x_in[1][:, t : t + 2, lo:hi].rearrange("p t n -> p n t"))
+
+        def quantize(s, lo=0, hi=N):
             nc.vector.quantize_mx(
-                out=codes[s][:].bitcast(FP8X4),
-                scales=xscale[s][:],
-                in_=x_bf[s][:].rearrange("p n t -> p (n t)"),
+                out=codes[s][:, lo:hi].bitcast(FP8X4),
+                scales=xscale[s][:, lo:hi],
+                in_=x_bf[s][:, lo:hi, :].rearrange("p n t -> p (n t)"),
             )
 
         def multiply(s):
-            for h in range(HALVES):
-                for c in range(SIDE):
+            for c in range(SIDE):
+                for h in range(HALVES):
                     rows = slice(ROWS * c, ROWS * (c + 1))
                     nc.tensor.matmul_mx(
                         out=acc[SIDE * s + c][h][:],
@@ -97,9 +103,12 @@ def tile_rows_glin_silu_bias_res_kernel(tc, x, w_words, w_scales, b, r, out):
 
         def finish(g):
             for h in range(HALVES):
-                nc.scalar.activation(out=act[:, g, h, :], in_=acc[g][h][:], func=SILU, bias=bias[:, g, h : h + 1])
+                nc.scalar.activation(out=act[:, g, h, :], in_=acc[g][h][:], func=SILU, bias=bias[:, h, 8 * g : 8 * g + 1])
                 nc.vector.tensor_tensor(out=res[:, g, h, :], in0=act[:, g, h, :], in1=r_in[:, g, h, :], op=ADD)
-            nc.sync.dma_start(out=out_v[:, g], in_=res[:, g])
+                if g == G - 1:
+                    nc.sync.dma_start(out=out_v[:, g, h], in_=res[:, g, h])
+            if g < G - 1:
+                nc.sync.dma_start(out=out_v[:, g], in_=res[:, g])
 
         nc.vector.tensor_copy(
             out=words[:].rearrange("p h s (q y) -> p h (s q) y", y=2),
@@ -113,9 +122,15 @@ def tile_rows_glin_silu_bias_res_kernel(tc, x, w_words, w_scales, b, r, out):
         )
         quantize(0)
         multiply(0)
-        interleave(1, nc.vector.tensor_copy, 0, VECTOR_COLUMNS)
-        interleave(1, nc.scalar.copy, VECTOR_COLUMNS, N)
-        quantize(1)
+        nc.vector.tensor_copy(out=bias_dealt[:], in_=bias_in[:].rearrange("p (a h) -> p h a", h=HALVES))
+        for h in range(HALVES):
+            nc.vector.transpose(out=bias[:, h, :], in_=bias_dealt[:, h, :])
+        pair_copy(nc.scalar.copy, 0, 0, 384)
+        pair_copy(nc.vector.tensor_copy, 0, 384, N)
+        for lo in (0, N // 2):
+            pair_copy(nc.vector.tensor_copy, 2, lo, lo + N // 2)
+        for lo in (0, N // 2):
+            quantize(1, lo, lo + N // 2)
         multiply(1)
         for g in range(G):
             finish(g)

@@ -20,7 +20,7 @@ ROWS = D // PACK
 SIDE = P // ROWS
 PAIRS = G // SIDE
 HALVES = M // P
-VECTOR_COLUMNS = 352
+VECTOR_COLUMNS = 336
 
 
 def tile_rows_glin_silu_bias_res_kernel(tc, x, w_words, w_scales, b, r, out):
@@ -37,8 +37,7 @@ def tile_rows_glin_silu_bias_res_kernel(tc, x, w_words, w_scales, b, r, out):
         bias_in = sb.tile([P, 64], F32, align_bytes=64)
         bias_dealt = sb.tile([P, HALVES, 32], F32, align_bytes=64)
         bias = sb.tile([P, HALVES, 32], F32, align_bytes=64)
-        warm = sb.tile([P, 8], F32)
-        warm_out = sb.tile([P, 8], F32)
+        zeros = sb.tile([P, 64], F32)
         x_in = [sb.tile([P, PACK, N], F32, name="x_in%d" % s, align_bytes=64) for s in range(PAIRS)]
         x_bf = [sb.tile([P, N, PACK], BF16, name="x_bf%d" % s, align_bytes=64) for s in range(PAIRS)]
         codes = [sb.tile([P, N], U32, name="codes%d" % s, align_bytes=64) for s in range(PAIRS)]
@@ -53,9 +52,9 @@ def tile_rows_glin_silu_bias_res_kernel(tc, x, w_words, w_scales, b, r, out):
         out_v = out.rearrange("g (p h) n -> p g h n", h=HALVES)
         scale_v = w_scales.rearrange("(s c) (q i) m -> i (c q) s m", c=SIDE, i=4)
 
+        nc.vector.memset(zeros[:], 0.0)
         nc.vector.memset(wscale_in[:].bitcast(I32), 0)
-        nc.vector.memset(warm[:], 0.0)
-        nc.vector.memset(bias_in[:], 0.0)
+        nc.scalar.activation(out=bias_in[:], in_=zeros[:], func=SILU)
 
         nc.sync.dma_start(
             out=words_in[:].bitcast(I32),
@@ -69,7 +68,6 @@ def tile_rows_glin_silu_bias_res_kernel(tc, x, w_words, w_scales, b, r, out):
             nc.sync.dma_start(out=x_in[1][:, lo : lo + 2], in_=x_v[1][:, lo : lo + 2])
         for lo, hi in ((0, 1), (1, 2), (2, 3), (3, 4)):
             nc.sync.dma_start(out=r_in[:, lo:hi], in_=r_v[:, lo:hi])
-        nc.scalar.activation(out=warm_out[:], in_=warm[:], func=SILU)
 
         def interleave(s, engine_copy, lo, hi):
             engine_copy(
@@ -101,14 +99,15 @@ def tile_rows_glin_silu_bias_res_kernel(tc, x, w_words, w_scales, b, r, out):
                         stop=True,
                     )
 
+        def activate(g, h):
+            nc.scalar.activation(out=act[:, g, h, :], in_=acc[g][h][:], func=SILU, bias=bias[:, h, 8 * g : 8 * g + 1])
+
         def finish(g):
             for h in range(HALVES):
-                nc.scalar.activation(out=act[:, g, h, :], in_=acc[g][h][:], func=SILU, bias=bias[:, h, 8 * g : 8 * g + 1])
+                if (g, h) != (0, 0):
+                    activate(g, h)
                 nc.vector.tensor_tensor(out=res[:, g, h, :], in0=act[:, g, h, :], in1=r_in[:, g, h, :], op=ADD)
-                if g == G - 1:
-                    nc.sync.dma_start(out=out_v[:, g, h], in_=res[:, g, h])
-            if g < G - 1:
-                nc.sync.dma_start(out=out_v[:, g], in_=res[:, g])
+            nc.sync.dma_start(out=out_v[:, g], in_=res[:, g])
 
         nc.vector.tensor_copy(
             out=words[:].rearrange("p h s (q y) -> p h (s q) y", y=2),
@@ -125,10 +124,13 @@ def tile_rows_glin_silu_bias_res_kernel(tc, x, w_words, w_scales, b, r, out):
         nc.vector.tensor_copy(out=bias_dealt[:], in_=bias_in[:].rearrange("p (a h) -> p h a", h=HALVES))
         for h in range(HALVES):
             nc.vector.transpose(out=bias[:, h, :], in_=bias_dealt[:, h, :])
-        pair_copy(nc.scalar.copy, 0, 0, 384)
-        pair_copy(nc.vector.tensor_copy, 0, 384, N)
-        for lo in (0, N // 2):
-            pair_copy(nc.vector.tensor_copy, 2, lo, lo + N // 2)
+        pair_copy(nc.scalar.copy, 0, 0, 256)
+        pair_copy(nc.vector.tensor_copy, 0, 256, N)
+
+        pair_copy(nc.vector.tensor_copy, 2, 0, N // 2)
+        pair_copy(nc.vector.tensor_copy, 2, N // 2, 384)
+        pair_copy(nc.scalar.copy, 2, 384, N)
+        activate(0, 0)
         for lo in (0, N // 2):
             quantize(1, lo, lo + N // 2)
         multiply(1)

@@ -14,13 +14,23 @@ ADD = mybir.AluOpType.add
 
 G, D, M, N = 4, 256, 256, 512
 FLOPS = 2 * G * D * M * N
+
 P = 128
+QUAD = 32
+QUADS = P // QUAD
 PACK = 4
 ROWS = D // PACK
 SIDE = P // ROWS
 PAIRS = G // SIDE
 HALVES = M // P
-VECTOR_COLUMNS = 336
+SCALE_ROWS = 4
+W_BYTES = 2
+BIAS_STEP = QUAD // G
+RUN = 4
+
+FIRST_PAIR_SPLIT = 336
+EARLY_SPLIT = 320
+LATE_SPLIT = 384
 
 
 def tile_rows_glin_silu_bias_res_kernel(tc, x, w_words, w_scales, b, r, out):
@@ -30,14 +40,14 @@ def tile_rows_glin_silu_bias_res_kernel(tc, x, w_words, w_scales, b, r, out):
         ps = ctx.enter_context(tc.psum_pool(name="ps", bufs=1))
         ctx.enter_context(tc.manual_schedule())
 
-        words_in = sb.tile([P, PAIRS, 2 * M], U8, align_bytes=64)
-        words = sb.tile([P, HALVES, PAIRS, 2 * P], U8, align_bytes=64)
+        words_in = sb.tile([P, PAIRS, W_BYTES * M], U8, align_bytes=64)
+        words = sb.tile([P, HALVES, PAIRS, W_BYTES * P], U8, align_bytes=64)
         wscale_in = sb.tile([P, PAIRS, M], U8, align_bytes=64)
         wscale = sb.tile([P, HALVES, PAIRS, P], U8, align_bytes=64)
-        bias_in = sb.tile([P, 64], F32, align_bytes=64)
-        bias_dealt = sb.tile([P, HALVES, 32], F32, align_bytes=64)
-        bias = sb.tile([P, HALVES, 32], F32, align_bytes=64)
-        zeros = sb.tile([P, 64], F32)
+        bias_in = sb.tile([P, HALVES * QUAD], F32, align_bytes=64)
+        bias_dealt = sb.tile([P, HALVES, QUAD], F32, align_bytes=64)
+        bias = sb.tile([P, HALVES, QUAD], F32, align_bytes=64)
+        zeros = sb.tile([P, HALVES * QUAD], F32)
         x_in = [sb.tile([P, PACK, N], F32, name="x_in%d" % s, align_bytes=64) for s in range(PAIRS)]
         x_bf = [sb.tile([P, N, PACK], BF16, name="x_bf%d" % s, align_bytes=64) for s in range(PAIRS)]
         codes = [sb.tile([P, N], U32, name="codes%d" % s, align_bytes=64) for s in range(PAIRS)]
@@ -50,35 +60,36 @@ def tile_rows_glin_silu_bias_res_kernel(tc, x, w_words, w_scales, b, r, out):
         x_v = x.rearrange("(s c) (p j) n -> s (c p) j n", c=SIDE, j=PACK)
         r_v = r.rearrange("g (p h) n -> p g h n", h=HALVES)
         out_v = out.rearrange("g (p h) n -> p g h n", h=HALVES)
-        scale_v = w_scales.rearrange("(s c) (q i) m -> i (c q) s m", c=SIDE, i=4)
+        scale_v = w_scales.rearrange("(s c) (q i) m -> i (c q) s m", c=SIDE, i=SCALE_ROWS)
 
         nc.vector.memset(zeros[:], 0.0)
         nc.vector.memset(wscale_in[:].bitcast(I32), 0)
         nc.scalar.activation(out=bias_in[:], in_=zeros[:], func=SILU)
 
+        early, late = slice(0, PACK // 2), slice(PACK // 2, PACK)
         nc.sync.dma_start(
             out=words_in[:].bitcast(I32),
             in_=w_words.rearrange("(s c) p y -> (c p) s y", c=SIDE).bitcast(I32),
         )
         nc.sync.dma_start(out=x_in[0][:], in_=x_v[0])
-        for i in range(4):
-            nc.sync.dma_start(out=wscale_in[i:P:32].bitcast(I32), in_=scale_v[i].bitcast(I32))
-        nc.sync.dma_start(out=bias_in[0:P:8, :], in_=b.rearrange("g (q j) o -> q g (j o)", q=4))
-        for lo in (0, 2):
-            nc.sync.dma_start(out=x_in[1][:, lo : lo + 2], in_=x_v[1][:, lo : lo + 2])
-        for lo, hi in ((0, 1), (1, 2), (2, 3), (3, 4)):
-            nc.sync.dma_start(out=r_in[:, lo:hi], in_=r_v[:, lo:hi])
+        for i in range(SCALE_ROWS):
+            nc.sync.dma_start(out=wscale_in[i:P:QUAD].bitcast(I32), in_=scale_v[i].bitcast(I32))
+        nc.sync.dma_start(out=x_in[1][:, early], in_=x_v[1][:, early])
+        nc.sync.dma_start(out=bias_in[0:P:BIAS_STEP, :], in_=b.rearrange("g (q j) o -> q g (j o)", q=QUADS))
+        nc.sync.dma_start(out=x_in[1][:, late], in_=x_v[1][:, late])
+        for g in range(G):
+            nc.sync.dma_start(out=r_in[:, g : g + 1], in_=r_v[:, g : g + 1])
 
-        def interleave(s, engine_copy, lo, hi):
-            engine_copy(
-                out=x_bf[s][:, lo:hi, :].rearrange("p (c i) t -> p c t i", i=4),
-                in_=x_in[s][:, :, lo:hi].rearrange("p t (c i) -> p c t i", i=4),
+        def cast_first_pair(copy, lo, hi):
+            copy(
+                out=x_bf[0][:, lo:hi, :].rearrange("p (u i) t -> p u t i", i=RUN),
+                in_=x_in[0][:, :, lo:hi].rearrange("p t (u i) -> p u t i", i=RUN),
             )
 
-        def pair_copy(engine_copy, t, lo, hi):
-            engine_copy(out=x_bf[1][:, lo:hi, t : t + 2], in_=x_in[1][:, t : t + 2, lo:hi].rearrange("p t n -> p n t"))
+        def cast_second_pair(copy, feats, lo, hi):
+            copy(out=x_bf[1][:, lo:hi, feats], in_=x_in[1][:, feats, lo:hi].rearrange("p t n -> p n t"))
 
-        def quantize(s, lo=0, hi=N):
+        def quantize(s, lo, hi):
             nc.vector.quantize_mx(
                 out=codes[s][:, lo:hi].bitcast(FP8X4),
                 scales=xscale[s][:, lo:hi],
@@ -87,8 +98,8 @@ def tile_rows_glin_silu_bias_res_kernel(tc, x, w_words, w_scales, b, r, out):
 
         def multiply(s):
             for c in range(SIDE):
+                rows = slice(ROWS * c, ROWS * (c + 1))
                 for h in range(HALVES):
-                    rows = slice(ROWS * c, ROWS * (c + 1))
                     nc.tensor.matmul_mx(
                         out=acc[SIDE * s + c][h][:],
                         lhsT=words[rows, h, s, :].bitcast(FP4X4),
@@ -99,40 +110,40 @@ def tile_rows_glin_silu_bias_res_kernel(tc, x, w_words, w_scales, b, r, out):
                         stop=True,
                     )
 
-        def activate(g, h):
-            nc.scalar.activation(out=act[:, g, h, :], in_=acc[g][h][:], func=SILU, bias=bias[:, h, 8 * g : 8 * g + 1])
-
-        def finish(g):
-            for h in range(HALVES):
-                if (g, h) != (0, 0):
-                    activate(g, h)
-                nc.vector.tensor_tensor(out=res[:, g, h, :], in0=act[:, g, h, :], in1=r_in[:, g, h, :], op=ADD)
-            nc.sync.dma_start(out=out_v[:, g], in_=res[:, g])
-
         nc.vector.tensor_copy(
-            out=words[:].rearrange("p h s (q y) -> p h (s q) y", y=2),
-            in_=words_in[:].rearrange("p s (q h y) -> p h (s q) y", h=HALVES, y=2),
+            out=words[:].rearrange("p h s (k y) -> p h (s k) y", y=W_BYTES),
+            in_=words_in[:].rearrange("p s (k h y) -> p h (s k) y", h=HALVES, y=W_BYTES),
         )
-        interleave(0, nc.vector.tensor_copy, 0, VECTOR_COLUMNS)
-        interleave(0, nc.scalar.copy, VECTOR_COLUMNS, N)
+        cast_first_pair(nc.vector.tensor_copy, 0, FIRST_PAIR_SPLIT)
+        cast_first_pair(nc.scalar.copy, FIRST_PAIR_SPLIT, N)
         nc.vector.tensor_copy(
-            out=wscale[:].rearrange("p h s q -> p h (s q)"),
-            in_=wscale_in[:].rearrange("p s (q h) -> p h (s q)", h=HALVES),
+            out=wscale[:].rearrange("p h s k -> p h (s k)"),
+            in_=wscale_in[:].rearrange("p s (k h) -> p h (s k)", h=HALVES),
         )
-        quantize(0)
+        quantize(0, 0, N)
         multiply(0)
-        nc.vector.tensor_copy(out=bias_dealt[:], in_=bias_in[:].rearrange("p (a h) -> p h a", h=HALVES))
+
+        nc.scalar.copy(out=bias_dealt[:], in_=bias_in[:].rearrange("p (a h) -> p h a", h=HALVES))
         for h in range(HALVES):
             nc.vector.transpose(out=bias[:, h, :], in_=bias_dealt[:, h, :])
-        pair_copy(nc.scalar.copy, 0, 0, 256)
-        pair_copy(nc.vector.tensor_copy, 0, 256, N)
 
-        pair_copy(nc.vector.tensor_copy, 2, 0, N // 2)
-        pair_copy(nc.vector.tensor_copy, 2, N // 2, 384)
-        pair_copy(nc.scalar.copy, 2, 384, N)
-        activate(0, 0)
+        cast_second_pair(nc.scalar.copy, early, 0, EARLY_SPLIT)
+        cast_second_pair(nc.vector.tensor_copy, early, EARLY_SPLIT, N)
+        cast_second_pair(nc.vector.tensor_copy, late, 0, N // 2)
+        cast_second_pair(nc.vector.tensor_copy, late, N // 2, LATE_SPLIT)
+        cast_second_pair(nc.scalar.copy, late, LATE_SPLIT, N)
         for lo in (0, N // 2):
             quantize(1, lo, lo + N // 2)
         multiply(1)
+
         for g in range(G):
-            finish(g)
+            for h in range(HALVES):
+                column = BIAS_STEP * g
+                nc.scalar.activation(
+                    out=act[:, g, h, :], in_=acc[g][h][:], func=SILU, bias=bias[:, h, column : column + 1]
+                )
+                nc.vector.tensor_tensor(out=res[:, g, h, :], in0=act[:, g, h, :], in1=r_in[:, g, h, :], op=ADD)
+                if g == G - 1:
+                    nc.sync.dma_start(out=out_v[:, g, h], in_=res[:, g, h])
+            if g < G - 1:
+                nc.sync.dma_start(out=out_v[:, g], in_=res[:, g])

from contextlib import ExitStack

import concourse.mybir as mybir

F32 = mybir.dt.float32
BF16 = mybir.dt.bfloat16
I32 = mybir.dt.int32
U32 = mybir.dt.uint32
U8 = mybir.dt.uint8
FP8X4 = mybir.dt.float8_e4m3fn_x4
FP4X4 = mybir.dt.float4_e2m1fn_x4
SILU = mybir.ActivationFunctionType.Silu
ADD = mybir.AluOpType.add

G, D, M, N = 4, 256, 256, 512
FLOPS = 2 * G * D * M * N

P = 128
QUAD = 32
QUADS = P // QUAD
PACK = 4
ROWS = D // PACK
SIDE = P // ROWS
PAIRS = G // SIDE
HALVES = M // P
SCALE_ROWS = 4
W_BYTES = 2
BIAS_STEP = QUAD // G
RUN = 4

FIRST_PAIR_SPLIT = 336
EARLY_SPLIT = 320
LATE_SPLIT = 384


def tile_rows_glin_silu_bias_res_kernel(tc, x, w_words, w_scales, b, r, out):
    nc = tc.nc
    with ExitStack() as ctx:
        sb = ctx.enter_context(tc.tile_pool(name="sb", bufs=1))
        ps = ctx.enter_context(tc.psum_pool(name="ps", bufs=1))
        ctx.enter_context(tc.manual_schedule())

        words_in = sb.tile([P, PAIRS, W_BYTES * M], U8, align_bytes=64)
        words = sb.tile([P, HALVES, PAIRS, W_BYTES * P], U8, align_bytes=64)
        wscale_in = sb.tile([P, PAIRS, M], U8, align_bytes=64)
        wscale = sb.tile([P, HALVES, PAIRS, P], U8, align_bytes=64)
        bias_in = sb.tile([P, HALVES * QUAD], F32, align_bytes=64)
        bias_dealt = sb.tile([P, HALVES, QUAD], F32, align_bytes=64)
        bias = sb.tile([P, HALVES, QUAD], F32, align_bytes=64)
        zeros = sb.tile([P, HALVES * QUAD], F32)
        x_in = [sb.tile([P, PACK, N], F32, name="x_in%d" % s, align_bytes=64) for s in range(PAIRS)]
        x_bf = [sb.tile([P, N, PACK], BF16, name="x_bf%d" % s, align_bytes=64) for s in range(PAIRS)]
        codes = [sb.tile([P, N], U32, name="codes%d" % s, align_bytes=64) for s in range(PAIRS)]
        xscale = [sb.tile([P, N], U8, name="xscale%d" % s, align_bytes=64) for s in range(PAIRS)]
        r_in = sb.tile([P, G, HALVES, N], F32)
        act = sb.tile([P, G, HALVES, N], F32)
        res = sb.tile([P, G, HALVES, N], F32)
        acc = [[ps.tile([P, N], F32, name="acc%d_%d" % (g, h)) for h in range(HALVES)] for g in range(G)]

        x_v = x.rearrange("(s c) (p j) n -> s (c p) j n", c=SIDE, j=PACK)
        r_v = r.rearrange("g (p h) n -> p g h n", h=HALVES)
        out_v = out.rearrange("g (p h) n -> p g h n", h=HALVES)
        scale_v = w_scales.rearrange("(s c) (q i) m -> i (c q) s m", c=SIDE, i=SCALE_ROWS)

        nc.vector.memset(zeros[:], 0.0)
        nc.vector.memset(wscale_in[:].bitcast(I32), 0)
        nc.scalar.activation(out=bias_in[:], in_=zeros[:], func=SILU)

        early, late = slice(0, PACK // 2), slice(PACK // 2, PACK)
        nc.sync.dma_start(
            out=words_in[:].bitcast(I32),
            in_=w_words.rearrange("(s c) p y -> (c p) s y", c=SIDE).bitcast(I32),
        )
        nc.sync.dma_start(out=x_in[0][:], in_=x_v[0])
        for i in range(SCALE_ROWS):
            nc.sync.dma_start(out=wscale_in[i:P:QUAD].bitcast(I32), in_=scale_v[i].bitcast(I32))
        nc.sync.dma_start(out=x_in[1][:, early], in_=x_v[1][:, early])
        nc.sync.dma_start(out=bias_in[0:P:BIAS_STEP, :], in_=b.rearrange("g (q j) o -> q g (j o)", q=QUADS))
        nc.sync.dma_start(out=x_in[1][:, late], in_=x_v[1][:, late])
        for g in range(G):
            nc.sync.dma_start(out=r_in[:, g : g + 1], in_=r_v[:, g : g + 1])

        def cast_first_pair(copy, lo, hi):
            copy(
                out=x_bf[0][:, lo:hi, :].rearrange("p (u i) t -> p u t i", i=RUN),
                in_=x_in[0][:, :, lo:hi].rearrange("p t (u i) -> p u t i", i=RUN),
            )

        def cast_second_pair(copy, feats, lo, hi):
            copy(out=x_bf[1][:, lo:hi, feats], in_=x_in[1][:, feats, lo:hi].rearrange("p t n -> p n t"))

        def quantize(s, lo, hi):
            nc.vector.quantize_mx(
                out=codes[s][:, lo:hi].bitcast(FP8X4),
                scales=xscale[s][:, lo:hi],
                in_=x_bf[s][:, lo:hi, :].rearrange("p n t -> p (n t)"),
            )

        def multiply(s):
            for c in range(SIDE):
                rows = slice(ROWS * c, ROWS * (c + 1))
                for h in range(HALVES):
                    nc.tensor.matmul_mx(
                        out=acc[SIDE * s + c][h][:],
                        lhsT=words[rows, h, s, :].bitcast(FP4X4),
                        lhsT_scale=wscale[rows, h, s, :],
                        rhs=codes[s][rows, :].bitcast(FP8X4),
                        rhs_scale=xscale[s][rows, :],
                        start=True,
                        stop=True,
                    )

        nc.vector.tensor_copy(
            out=words[:].rearrange("p h s (k y) -> p h (s k) y", y=W_BYTES),
            in_=words_in[:].rearrange("p s (k h y) -> p h (s k) y", h=HALVES, y=W_BYTES),
        )
        cast_first_pair(nc.vector.tensor_copy, 0, FIRST_PAIR_SPLIT)
        cast_first_pair(nc.scalar.copy, FIRST_PAIR_SPLIT, N)
        nc.vector.tensor_copy(
            out=wscale[:].rearrange("p h s k -> p h (s k)"),
            in_=wscale_in[:].rearrange("p s (k h) -> p h (s k)", h=HALVES),
        )
        quantize(0, 0, N)
        multiply(0)

        nc.scalar.copy(out=bias_dealt[:], in_=bias_in[:].rearrange("p (a h) -> p h a", h=HALVES))
        for h in range(HALVES):
            nc.vector.transpose(out=bias[:, h, :], in_=bias_dealt[:, h, :])

        cast_second_pair(nc.scalar.copy, early, 0, EARLY_SPLIT)
        cast_second_pair(nc.vector.tensor_copy, early, EARLY_SPLIT, N)
        cast_second_pair(nc.vector.tensor_copy, late, 0, N // 2)
        cast_second_pair(nc.vector.tensor_copy, late, N // 2, LATE_SPLIT)
        cast_second_pair(nc.scalar.copy, late, LATE_SPLIT, N)
        for lo in (0, N // 2):
            quantize(1, lo, lo + N // 2)
        multiply(1)

        for g in range(G):
            for h in range(HALVES):
                column = BIAS_STEP * g
                nc.scalar.activation(
                    out=act[:, g, h, :], in_=acc[g][h][:], func=SILU, bias=bias[:, h, column : column + 1]
                )
                nc.vector.tensor_tensor(out=res[:, g, h, :], in0=act[:, g, h, :], in1=r_in[:, g, h, :], op=ADD)
                if g == G - 1:
                    nc.sync.dma_start(out=out_v[:, g, h], in_=res[:, g, h])
            if g < G - 1:
                nc.sync.dma_start(out=out_v[:, g], in_=res[:, g])
